import numpy as np
import ml_dtypes


def mxq(x, axis, fmt="e4m3"):
    dtype, down = {"e4m3": (ml_dtypes.float8_e4m3fn, 7), "e5m2": (ml_dtypes.float8_e5m2, 14)}[fmt]
    v = np.moveaxis(np.asarray(x, np.float32).astype(ml_dtypes.bfloat16).astype(np.float64), axis, -1)
    blocks = v.reshape(v.shape[:-1] + (-1, 32))
    amax = np.abs(blocks).max(-1, keepdims=True)
    byte = np.maximum(np.where(amax > 0, np.frexp(amax)[1] - 1 + 127, 0) - down, 1)
    scale = np.exp2(byte - 127.0)
    codes = (blocks / scale).astype(np.float32).astype(dtype).astype(np.float64)
    return np.moveaxis((codes * scale).reshape(v.shape), -1, axis)


WIDE = False


def mx_kscale(k):
    if not WIDE:
        return np.ones(k)
    levels = np.array([10, -10, 5, -5, 0])
    if k % 512:
        return np.exp2(np.random.permutation(np.resize(levels, k // 32))).repeat(32)
    a = np.empty((k // 512, 16))
    for p in range(k // 512):
        a[p, :8] = np.random.permutation(np.resize(levels, 8))
        for g in range(8):
            far = levels[np.abs(levels - a[p, g]) >= 10]
            a[p, g + 8] = far[np.random.randint(len(far))]
    return np.exp2(a.ravel()).repeat(32)


def f64(x):
    return np.asarray(x).astype(np.float64)


def striped(idx):
    return np.tile(idx.reshape(-1, 16).T, (8, 1)).astype(np.uint16)


def unstriped(offs):
    return offs[:16].T.reshape(-1).astype(np.int64)


def striped8(idx):
    return np.concatenate([x.reshape(-1, 16).T for x in idx]).astype(np.uint16)


def runs(offs, k):
    lists = np.stack([offs[16 * r : 16 * r + 16].T.reshape(-1) for r in range(8)]).astype(np.int64)
    return lists[np.arange(k) % 512 // 64]


def pack_weight(w):
    k, n = w.shape
    w = f64(np.asarray(w, np.float32).astype(ml_dtypes.bfloat16)).reshape(k // 32, 32, n)
    amax = np.abs(w).max(1)
    byte = np.clip(np.where(amax > 0, np.frexp(amax)[1] - 1 + 127 - 7, 1), 1, 254)
    scaled = (w * np.exp2(127.0 - byte)[:, None, :]).reshape(k, n).astype(np.float32)
    words = np.ascontiguousarray(scaled.reshape(k // 512, 128, 4, n).transpose(0, 1, 3, 2)).astype(ml_dtypes.float8_e4m3fn).view(np.uint8)
    return words, np.ascontiguousarray(byte.astype(np.uint8).reshape(k // 512, 16, n))


def unpack_weight(words, scales):
    g, p, n, _ = words.shape
    vals = np.ascontiguousarray(words).view(ml_dtypes.float8_e4m3fn).astype(np.float64) * np.repeat(np.exp2(scales.astype(np.float64) - 127.0), 8, axis=1)[..., None]
    return vals.transpose(0, 1, 3, 2).reshape(g * 512, n)

def planes(y):
    n, m = y.shape
    v = y.astype(np.float32).astype(ml_dtypes.bfloat16).astype(np.float64).reshape(n // 32, 32, m)
    top = np.abs(v).max(1)
    byte = np.clip(np.where(top > 0, np.frexp(top)[1] - 1 + 127 - 7, 1), 1, 254)
    codes = (v * np.exp2(127.0 - byte)[:, None, :]).reshape(n, m).astype(np.float32).astype(ml_dtypes.float8_e4m3fn).view(np.uint8)
    words = codes.reshape(n // 512, 128, 4, m).transpose(0, 1, 3, 2)
    return np.ascontiguousarray(words), np.ascontiguousarray(byte.astype(np.uint8).reshape(n // 512, 16, m))


K, T, S, N, G, H = 512, 2048, 512, 512, 2048, 512


def setup_inputs():
    n = np.random.standard_normal
    s = mx_kscale(K)[:, None]
    u = mx_kscale(S)
    packed_xT = pack_weight(n((K, T)) * s)
    packed_dT = pack_weight(n((K, G)) / s)
    packed_w1 = pack_weight(n((H, N)) / np.sqrt(H) / u[:, None])
    return {
        "x_words": packed_xT[0],
        "x_scales": packed_xT[1],
        "d_words": packed_dT[0],
        "d_scales": packed_dT[1],
        "gn": (np.random.uniform(0.5, 1.5, (H, 1)) * u[:, None]).astype(np.float32),
        "w1_words": packed_w1[0],
        "w1_scales": packed_w1[1],
        "offs": striped(np.random.permutation(T)[:S]),
        "kidx": striped8(np.random.randint(0, G, (8, H))),
        "n1": striped8(np.stack([np.random.permutation(S) for _ in range(8)])),
        "n2": striped8(np.stack([np.random.permutation(S) for _ in range(8)])),
        "n3": striped8(np.stack([np.random.permutation(S) for _ in range(8)])),
        "n4": striped8(np.stack([np.random.permutation(S) for _ in range(8)])),
    }


def reference(x_words, x_scales, d_words, d_scales, gn, w1_words, w1_scales, offs, kidx, n1, n2, n3, n4):
    d_kidx = unpack_weight(d_words, d_scales)[np.arange(K)[:, None], runs(kidx, K)]
    xq = unpack_weight(x_words, x_scales)[:, unstriped(offs)]
    s = 0.0625 * (d_kidx.T @ xq)
    pa = s[np.arange(H)[:, None], runs(n1, H)]
    z = f64(gn) * ((2.0 * (s * pa)) / ((s) ** 2 + (pa) ** 2 + 0.5))
    h = unpack_weight(w1_words, w1_scales).T @ mxq(z, 0, "e4m3")
    out_0 = 0.75 * (h * (h[np.arange(N)[:, None], runs(n2, N)]) + (h[np.arange(N)[:, None], runs(n3, N)]) * (h[np.arange(N)[:, None], runs(n4, N)]))
    return (out_0,) + planes(out_0)

@@ -1,0 +1,277 @@
+import math
+from contextlib import ExitStack
+
+import concourse.mybir as mybir
+
+K, T, S, N, G, H = 512, 2048, 512, 512, 2048, 512
+FLOPS = 2 * K * H * S + 2 * H * N * S
+
+F32 = mybir.dt.float32
+BF16 = mybir.dt.bfloat16
+I32 = mybir.dt.int32
+U32 = mybir.dt.uint32
+U16 = mybir.dt.uint16
+U8 = mybir.dt.uint8
+FP8X4 = mybir.dt.float8_e4m3fn_x4
+MULT = mybir.AluOpType.mult
+ADD = mybir.AluOpType.add
+ACT = mybir.ActivationFunctionType
+
+P = 128
+PACK = 4
+SCORE_SCALE = 0.0625
+ROOT_OUT_SCALE = math.sqrt(0.75)
+Z_CHUNKS = ((0, 256), (256, 384), (384, 512))
+OUT_CHUNKS = ((0, 128), (128, 256), (256, 384), (384, 512))
+
+
+def words_of(dram):
+    return dram[0].rearrange("p n t -> p (n t)").bitcast(I32)
+
+
+def entries(lst, a, b):
+    return lst[:, a // 16 : b // 16]
+
+
+def walk_out(ap):
+    return ap.rearrange("p (c i t) -> p c t i", i=4, t=PACK)
+
+
+def walk_in(ap):
+    return ap.rearrange("p t (c i) -> p c t i", i=4)
+
+
+def tile_picked_keyharmdot_none_po_kernel(
+    tc, x_words, x_scales, d_words, d_scales, gn, w1_words, w1_scales, offs, kidx, n1, n2, n3, n4, out_0, out_1, out_2
+):
+    nc = tc.nc
+    with ExitStack() as ctx:
+        lists = ctx.enter_context(tc.tile_pool(name="lists", bufs=1))
+        keep = ctx.enter_context(tc.tile_pool(name="keep", bufs=1))
+        psum = ctx.enter_context(tc.psum_pool(name="psum", bufs=1))
+
+        def sb(name, cols, dtype):
+            return keep.tile([P] + list(cols), dtype, name=name, align_bytes=64)
+
+        kidx_sb = lists.tile([P, H // 16], U16, name="kidx_sb")
+        offs_sb = lists.tile([P, S // 16], U16, name="offs_sb")
+        n1_sb = lists.tile([P, S // 16], U16, name="n1_sb")
+        n2_sb = lists.tile([P, S // 16], U16, name="n2_sb")
+        n3_sb = lists.tile([P, S // 16], U16, name="n3_sb")
+        n4_sb = lists.tile([P, S // 16], U16, name="n4_sb")
+
+        d_byte_table = sb("d_byte_table", [G], U8)
+        x_byte_table = sb("x_byte_table", [T], U8)
+        d_word_table = sb("d_word_table", [G], I32)
+        x_word_table = sb("x_word_table", [T], I32)
+        w_bytes_raw = sb("w_bytes_raw", [N], U8)
+        w_words_raw = sb("w_words_raw", [N], I32)
+        key_scales = sb("key_scales", [H], U8)
+        gn_sb = sb("gn_sb", [PACK], F32)
+        h_win = [sb("h_win%d" % t, [2 * S if t < PACK - 1 else S], F32) for t in range(PACK)]
+
+        nc.vector.memset(d_byte_table[:].bitcast(I32), 0)
+        nc.vector.memset(x_byte_table[:].bitcast(I32), 0)
+        nc.vector.memset(w_bytes_raw[:].bitcast(I32), 0)
+        nc.vector.memset(key_scales[:].bitcast(I32), 0)
+        for t in range(PACK - 1):
+            nc.vector.memset(h_win[t][:, S:], 0.0)
+
+        nc.sync.dma_start(kidx_sb[:], kidx)
+        nc.scalar.dma_start(d_byte_table[0:P:8, :].bitcast(I32), d_scales[0].bitcast(I32))
+        nc.sync.dma_start(offs_sb[:], offs)
+        nc.sync.dma_start(w_words_raw[:], words_of(w1_words))
+        nc.sync.dma_start(d_word_table[:], words_of(d_words))
+        for q in range(4):
+            nc.scalar.dma_start(x_byte_table[32 * q : 32 * q + 4, :].bitcast(I32), x_scales[0, 4 * q : 4 * q + 4, :].bitcast(I32))
+        nc.sync.dma_start(x_word_table[:], words_of(x_words))
+        nc.gpsimd.dma_start(gn_sb[:], gn.rearrange("(p t) o -> p (t o)", t=PACK))
+        for q in range(4):
+            nc.gpsimd.dma_start(w_bytes_raw[32 * q : 32 * q + 4, :].bitcast(I32), w1_scales[0, 4 * q : 4 * q + 4, :].bitcast(I32))
+        nc.sync.dma_start(n1_sb[:], n1)
+        nc.sync.dma_start(n3_sb[:], n3)
+        nc.sync.dma_start(n2_sb[:], n2)
+        nc.sync.dma_start(n4_sb[:], n4)
+
+        d_bytes_picked = sb("d_bytes_picked", [H], U8)
+        d_bytes_dealt = sb("d_bytes_dealt", [H], U8)
+        nc.vector.tensor_copy(d_bytes_picked[:], d_byte_table[:].indirect(kidx_sb[:]))
+        nc.vector.tensor_copy(
+            d_bytes_dealt[:].rearrange("p (t m) -> p m t", t=PACK), d_bytes_picked[:].rearrange("p (m t) -> p m t", t=PACK)
+        )
+        for q in range(4):
+            nc.scalar.dma_start(
+                key_scales[32 * q : 32 * q + 4, :].bitcast(I32), d_bytes_dealt[32 * q : 32 * q + 32 : 8, :].bitcast(I32)
+            )
+
+        gain = sb("gain", [PACK], F32)
+        nc.vector.tensor_scalar(gain[:], gn_sb[:], 2.0 * SCORE_SCALE, None, MULT)
+        warm = sb("warm", [1], F32)
+        nc.scalar.activation(warm[:], gn_sb[:, 0:1], ACT.Abs_reciprocal_sqrt)
+
+        query_scales = sb("query_scales", [S], U8)
+        nc.vector.tensor_copy(query_scales[:], x_byte_table[:].indirect(offs_sb[:]))
+
+        d_words_picked = sb("d_words_picked", [H], U32)
+        key_words = sb("key_words", [H], U32)
+        nc.vector.tensor_copy(d_words_picked[:], d_word_table[:].bitcast(U32).indirect(kidx_sb[:]))
+        nc.vector.tensor_copy(
+            key_words[:].bitcast(I32).rearrange("p (t m) -> p m t", t=PACK),
+            d_words_picked[:].bitcast(I32).rearrange("p (m t) -> p m t", t=PACK),
+        )
+
+        query_words = sb("query_words", [S], U32)
+        halves = ((0, S // 2), (S // 2, S))
+        for a, b in halves:
+            nc.vector.tensor_copy(query_words[:, a:b], x_word_table[:].bitcast(U32).indirect(entries(offs_sb, a, b)))
+
+        s_ps = [psum.tile([P, S], F32, name="s_ps%d" % t) for t in range(PACK)]
+        h_ps = [psum.tile([P, S], F32, name="h_ps%d" % t) for t in range(PACK)]
+        s_win = [sb("s_win%d" % t, [S], F32) for t in range(PACK)]
+
+        def score(t, a, b):
+            cols = slice(t * P, (t + 1) * P)
+            nc.tensor.matmul_mx(
+                out=s_ps[t][:, a:b], lhsT=key_words[:, cols].bitcast(FP8X4), lhsT_scale=key_scales[:, cols],
+                rhs=query_words[:, a:b].bitcast(FP8X4), rhs_scale=query_scales[:, a:b], start=True, stop=True,
+            )
+            nc.scalar.activation(s_win[t][:, a:b], s_ps[t][:, a:b], ACT.Copy, scale=SCORE_SCALE)
+
+        for t, half in ((0, 0), (1, 0), (0, 1), (1, 1), (2, 0), (2, 1), (3, 0), (3, 1)):
+            score(t, halves[half][0], halves[half][1])
+
+        value_words = sb("value_words", [N], U32)
+        value_scales = sb("value_scales", [N], U8)
+        nc.vector.tensor_copy(
+            value_words[:].bitcast(I32).rearrange("p (t m) -> p m t", t=PACK),
+            w_words_raw[:].rearrange("p (m t) -> p m t", t=PACK),
+        )
+        nc.vector.tensor_copy(
+            value_scales[:].rearrange("p (t m) -> p m t", t=PACK), w_bytes_raw[:].rearrange("p (m t) -> p m t", t=PACK)
+        )
+
+        z_words = sb("z_words", [S], U32)
+        z_scales = sb("z_scales", [S], U8)
+        st = {}
+        for c, (a, b) in enumerate(Z_CHUNKS):
+            for nm in ("pa", "s2", "p2", "den", "num", "root", "inv"):
+                st[nm, c] = sb("%s%d" % (nm, c), [PACK, b - a], F32)
+            st["z", c] = sb("z%d" % c, [(b - a) * PACK], BF16)
+
+        def flat(tile):
+            return tile[:].rearrange("p t c -> p (t c)")
+
+        def fetch(c):
+            a, b = Z_CHUNKS[c]
+            for t in range(PACK):
+                nc.vector.tensor_copy(st["pa", c][:, t, :], s_win[t][:].indirect(entries(n1_sb, a, b)))
+
+        def squares(c):
+            a, b = Z_CHUNKS[c]
+            for t in range(PACK):
+                nc.scalar.activation(st["s2", c][:, t, :], s_ps[t][:, a:b], ACT.Square, scale=SCORE_SCALE)
+            nc.scalar.activation(flat(st["p2", c]), flat(st["pa", c]), ACT.Square)
+
+        def denominator(c):
+            nc.vector.tensor_tensor(flat(st["den", c]), flat(st["s2", c]), flat(st["p2", c]), ADD)
+
+        def numerator(c):
+            a, b = Z_CHUNKS[c]
+            for t in range(PACK):
+                nc.vector.scalar_tensor_tensor(
+                    st["num", c][:, t, :], st["pa", c][:, t, :], gain[:, t : t + 1], s_ps[t][:, a:b], MULT, MULT
+                )
+
+        def inverse(c):
+            nc.scalar.activation(flat(st["root", c]), flat(st["den", c]), ACT.Abs_reciprocal_sqrt, bias=0.5)
+            nc.scalar.activation(flat(st["inv", c]), flat(st["root", c]), ACT.Square)
+
+        def quotient(c):
+            nc.vector.tensor_tensor(walk_out(st["z", c][:]), walk_in(st["num", c][:]), walk_in(st["inv", c][:]), MULT)
+
+        def quantise_z(c):
+            a, b = Z_CHUNKS[c]
+            nc.vector.quantize_mx(out=z_words[:, a:b].bitcast(FP8X4), scales=z_scales[:, a:b], in_=st["z", c][:])
+            for t in range(PACK):
+                cols = slice(t * P, (t + 1) * P)
+                nc.tensor.matmul_mx(
+                    out=h_ps[t][:, a:b], lhsT=value_words[:, cols].bitcast(FP8X4), lhsT_scale=value_scales[:, cols],
+                    rhs=z_words[:, a:b].bitcast(FP8X4), rhs_scale=z_scales[:, a:b], start=True, stop=True,
+                )
+
+        fetch(0)
+        squares(0)
+        fetch(1)
+        denominator(0)
+        squares(1)
+        fetch(2)
+        inverse(0)
+        denominator(1)
+        squares(2)
+        numerator(0)
+        inverse(1)
+        denominator(2)
+        quotient(0)
+        numerator(1)
+        inverse(2)
+        quantise_z(0)
+        numerator(2)
+        quotient(1)
+        quantise_z(1)
+        quotient(2)
+        quantise_z(2)
+
+        h_plain = [sb("h_plain%d" % t, [S], F32) for t in range(PACK)]
+
+        def h_out(t, a, b):
+            nc.scalar.activation(h_win[t][:, a:b], h_ps[t][:, a:b], ACT.Copy, scale=ROOT_OUT_SCALE)
+            nc.scalar.activation(h_plain[t][:, a:b], h_ps[t][:, a:b], ACT.Copy, scale=ROOT_OUT_SCALE)
+
+        split = Z_CHUNKS[-1][0]
+        h_out(0, 0, split)
+        h_out(0, split, S)
+        for t in range(1, PACK):
+            h_out(t, 0, S)
+
+        result = sb("result", [PACK, S], F32)
+        y_words = sb("y_words", [S], U32)
+        y_scales = sb("y_scales", [S], U8)
+        out_rows = out_0.rearrange("(p t) j -> p t j", t=PACK)
+        pieces = [(t, 0, S) for t in range(PACK - 1)] + [(PACK - 1, a, b) for a, b in OUT_CHUNKS]
+        prod = {}
+
+        def products(i):
+            t, a, b = pieces[i]
+            third = sb("third%d" % i, [b - a], F32)
+            first = sb("first%d" % i, [b - a], F32)
+            second = sb("second%d" % i, [b - a], F32)
+            prod[i] = (first, second)
+            nc.vector.tensor_copy(third[:], h_win[t][:].indirect(entries(n3_sb, a, b)))
+            nc.vector.tensor_tensor(first[:], h_win[t][:].indirect(entries(n2_sb, a, b)), h_plain[t][:, a:b], MULT)
+            if i > 0:
+                finish(i - 1)
+            nc.vector.tensor_tensor(second[:], h_win[t][:].indirect(entries(n4_sb, a, b)), third[:], MULT)
+            if i > 0:
+                planes(i - 1)
+
+        def finish(i):
+            t, a, b = pieces[i]
+            nc.vector.tensor_tensor(result[:, t, a:b], prod[i][0][:], prod[i][1][:], ADD)
+            nc.sync.dma_start(out_rows[:, t, a:b], result[:, t, a:b])
+            if t == PACK - 1:
+                prod[i, "y"] = sb("y%d" % i, [(b - a) * PACK], BF16)
+                nc.scalar.copy(walk_out(prod[i, "y"][:]), walk_in(result[:, :, a:b]))
+
+        def planes(i):
+            t, a, b = pieces[i]
+            if t == PACK - 1:
+                nc.vector.quantize_mx(out=y_words[:, a:b].bitcast(FP8X4), scales=y_scales[:, a:b], in_=prod[i, "y"][:])
+                nc.sync.dma_start(words_of(out_1)[:, a:b], y_words[:, a:b].bitcast(I32))
+
+        for i in range(len(pieces)):
+            products(i)
+        finish(len(pieces) - 1)
+        planes(len(pieces) - 1)
+        for q in range(4):
+            queue = nc.sync if q % 2 else nc.scalar
+            queue.dma_start(out_2[0, 4 * q : 4 * q + 4, :].bitcast(I32), y_scales[32 * q : 32 * q + 4, :].bitcast(I32))

@@ -2,6 +2,7 @@ import math
 from contextlib import ExitStack
 
 import concourse.mybir as mybir
+from concourse.masks import make_identity
 
 K, T, S, N, G, H = 512, 2048, 512, 512, 2048, 512
 FLOPS = 2 * K * H * S + 2 * H * N * S
@@ -21,8 +22,8 @@ P = 128
 PACK = 4
 SCORE_SCALE = 0.0625
 ROOT_OUT_SCALE = math.sqrt(0.75)
-Z_CHUNKS = ((0, 256), (256, 384), (384, 512))
-OUT_CHUNKS = ((0, 128), (128, 256), (256, 384), (384, 512))
+BLOCKS = S // P
+OUT_CHUNKS = ((0, 256), (256, 384), (384, 512))
 
 
 def words_of(dram):
@@ -41,6 +42,10 @@ def walk_in(ap):
     return ap.rearrange("p t (c i) -> p c t i", i=4)
 
 
+def block(c):
+    return slice(c * P, (c + 1) * P)
+
+
 def tile_picked_keyharmdot_none_po_kernel(
     tc, x_words, x_scales, d_words, d_scales, gn, w1_words, w1_scales, offs, kidx, n1, n2, n3, n4, out_0, out_1, out_2
 ):
@@ -50,8 +55,8 @@ def tile_picked_keyharmdot_none_po_kernel(
         keep = ctx.enter_context(tc.tile_pool(name="keep", bufs=1))
         psum = ctx.enter_context(tc.psum_pool(name="psum", bufs=1))
 
-        def sb(name, cols, dtype):
-            return keep.tile([P] + list(cols), dtype, name=name, align_bytes=64)
+        def sb(name, cols, dtype, tag=None):
+            return keep.tile([P] + list(cols), dtype, name=name, tag=tag or name, align_bytes=64)
 
         kidx_sb = lists.tile([P, H // 16], U16, name="kidx_sb")
         offs_sb = lists.tile([P, S // 16], U16, name="offs_sb")
@@ -62,36 +67,50 @@ def tile_picked_keyharmdot_none_po_kernel(
 
         d_byte_table = sb("d_byte_table", [G], U8)
         x_byte_table = sb("x_byte_table", [T], U8)
-        d_word_table = sb("d_word_table", [G], I32)
-        x_word_table = sb("x_word_table", [T], I32)
         w_bytes_raw = sb("w_bytes_raw", [N], U8)
-        w_words_raw = sb("w_words_raw", [N], I32)
         key_scales = sb("key_scales", [H], U8)
         gn_sb = sb("gn_sb", [PACK], F32)
+        ident = sb("ident", [P], F32)
         h_win = [sb("h_win%d" % t, [2 * S if t < PACK - 1 else S], F32) for t in range(PACK)]
 
-        nc.vector.memset(d_byte_table[:].bitcast(I32), 0)
+        warm_in = sb("warm_in", [1], F32, tag="x_words_slot")
+        warm_out = sb("warm_out", [1], F32)
+        half_src = sb("half_src", [1], F32, tag="d_words_slot")
+        bias_half = sb("bias_half", [1], F32)
+        nc.gpsimd.memset(d_byte_table[:].bitcast(I32), 0)
+        nc.vector.memset(half_src[:], 0.5)
+        nc.vector.tensor_copy(bias_half[:], half_src[:])
         nc.vector.memset(x_byte_table[:].bitcast(I32), 0)
-        nc.vector.memset(w_bytes_raw[:].bitcast(I32), 0)
-        nc.vector.memset(key_scales[:].bitcast(I32), 0)
+        nc.vector.memset(warm_in[:], 1.0)
+        score_scale = sb("score_scale", [1], F32, tag="late_slot")
+        nc.vector.memset(score_scale[:], SCORE_SCALE)
+        d_word_table = sb("d_word_table", [G], I32, tag="d_words_slot")
+        nc.gpsimd.memset(key_scales[:].bitcast(I32), 0)
+        nc.gpsimd.memset(w_bytes_raw[:].bitcast(I32), 0)
         for t in range(PACK - 1):
             nc.vector.memset(h_win[t][:, S:], 0.0)
+
 
         nc.sync.dma_start(kidx_sb[:], kidx)
         nc.scalar.dma_start(d_byte_table[0:P:8, :].bitcast(I32), d_scales[0].bitcast(I32))
         nc.sync.dma_start(offs_sb[:], offs)
-        nc.sync.dma_start(w_words_raw[:], words_of(w1_words))
         nc.sync.dma_start(d_word_table[:], words_of(d_words))
         for q in range(4):
-            nc.scalar.dma_start(x_byte_table[32 * q : 32 * q + 4, :].bitcast(I32), x_scales[0, 4 * q : 4 * q + 4, :].bitcast(I32))
-        nc.sync.dma_start(x_word_table[:], words_of(x_words))
+            queue = nc.scalar if q == 0 else nc.sync
+            queue.dma_start(x_byte_table[32 * q : 32 * q + 4, :].bitcast(I32), x_scales[0, 4 * q : 4 * q + 4, :].bitcast(I32))
+        nc.scalar.activation(warm_out[:], warm_in[:], ACT.Abs_reciprocal_sqrt)
+        x_word_table = sb("x_word_table", [T], I32, tag="x_words_slot")
+        nc.scalar.dma_start(x_word_table[:], words_of(x_words))
         nc.gpsimd.dma_start(gn_sb[:], gn.rearrange("(p t) o -> p (t o)", t=PACK))
+        gain = sb("gain", [PACK], F32)
+        nc.gpsimd.tensor_scalar(gain[:], gn_sb[:], 2.0 * SCORE_SCALE, 0.0, MULT, ADD)
         for q in range(4):
             nc.gpsimd.dma_start(w_bytes_raw[32 * q : 32 * q + 4, :].bitcast(I32), w1_scales[0, 4 * q : 4 * q + 4, :].bitcast(I32))
         nc.sync.dma_start(n1_sb[:], n1)
         nc.sync.dma_start(n3_sb[:], n3)
         nc.sync.dma_start(n2_sb[:], n2)
         nc.sync.dma_start(n4_sb[:], n4)
+        make_identity(nc, ident[:])
 
         d_bytes_picked = sb("d_bytes_picked", [H], U8)
         d_bytes_dealt = sb("d_bytes_dealt", [H], U8)
@@ -100,21 +119,17 @@ def tile_picked_keyharmdot_none_po_kernel(
             d_bytes_dealt[:].rearrange("p (t m) -> p m t", t=PACK), d_bytes_picked[:].rearrange("p (m t) -> p m t", t=PACK)
         )
         for q in range(4):
-            nc.scalar.dma_start(
+            nc.sync.dma_start(
                 key_scales[32 * q : 32 * q + 4, :].bitcast(I32), d_bytes_dealt[32 * q : 32 * q + 32 : 8, :].bitcast(I32)
             )
 
-        gain = sb("gain", [PACK], F32)
-        nc.vector.tensor_scalar(gain[:], gn_sb[:], 2.0 * SCORE_SCALE, None, MULT)
-        warm = sb("warm", [1], F32)
-        nc.scalar.activation(warm[:], gn_sb[:, 0:1], ACT.Abs_reciprocal_sqrt)
-
-        query_scales = sb("query_scales", [S], U8)
-        nc.vector.tensor_copy(query_scales[:], x_byte_table[:].indirect(offs_sb[:]))
-
+        w_words_raw = sb("w_words_raw", [N], I32, tag="d_bytes_picked")
+        nc.sync.dma_start(w_words_raw[:], words_of(w1_words))
         d_words_picked = sb("d_words_picked", [H], U32)
         key_words = sb("key_words", [H], U32)
         nc.vector.tensor_copy(d_words_picked[:], d_word_table[:].bitcast(U32).indirect(kidx_sb[:]))
+        query_scales = sb("query_scales", [S], U8)
+        nc.vector.tensor_copy(query_scales[:], x_byte_table[:].indirect(offs_sb[:]))
         nc.vector.tensor_copy(
             key_words[:].bitcast(I32).rearrange("p (t m) -> p m t", t=PACK),
             d_words_picked[:].bitcast(I32).rearrange("p (m t) -> p m t", t=PACK),
@@ -125,153 +140,172 @@ def tile_picked_keyharmdot_none_po_kernel(
         for a, b in halves:
             nc.vector.tensor_copy(query_words[:, a:b], x_word_table[:].bitcast(U32).indirect(entries(offs_sb, a, b)))
 
-        s_ps = [psum.tile([P, S], F32, name="s_ps%d" % t) for t in range(PACK)]
-        h_ps = [psum.tile([P, S], F32, name="h_ps%d" % t) for t in range(PACK)]
+        product_ps = [psum.tile([P, S], F32, name="product_ps%d" % t) for t in range(PACK)]
+        turned_ps = [psum.tile([P, PACK, P], F32, name="turned_ps%d" % i) for i in range(2)]
+        back_ps = [psum.tile([P, PACK, P], F32, name="back_ps%d" % i) for i in range(2)]
         s_win = [sb("s_win%d" % t, [S], F32) for t in range(PACK)]
 
         def score(t, a, b):
-            cols = slice(t * P, (t + 1) * P)
             nc.tensor.matmul_mx(
-                out=s_ps[t][:, a:b], lhsT=key_words[:, cols].bitcast(FP8X4), lhsT_scale=key_scales[:, cols],
+                out=product_ps[t][:, a:b], lhsT=key_words[:, block(t)].bitcast(FP8X4), lhsT_scale=key_scales[:, block(t)],
                 rhs=query_words[:, a:b].bitcast(FP8X4), rhs_scale=query_scales[:, a:b], start=True, stop=True,
             )
-            nc.scalar.activation(s_win[t][:, a:b], s_ps[t][:, a:b], ACT.Copy, scale=SCORE_SCALE)
+            nc.scalar.activation(s_win[t][:, a:b], product_ps[t][:, a:b], ACT.Copy, scale=score_scale[:])
 
         for t, half in ((0, 0), (1, 0), (0, 1), (1, 1), (2, 0), (2, 1), (3, 0), (3, 1)):
             score(t, halves[half][0], halves[half][1])
 
-        value_words = sb("value_words", [N], U32)
-        value_scales = sb("value_scales", [N], U8)
+        value_words = sb("value_words", [N], U32, tag="x_words_slot")
         nc.vector.tensor_copy(
             value_words[:].bitcast(I32).rearrange("p (t m) -> p m t", t=PACK),
             w_words_raw[:].rearrange("p (m t) -> p m t", t=PACK),
         )
-        nc.vector.tensor_copy(
-            value_scales[:].rearrange("p (t m) -> p m t", t=PACK), w_bytes_raw[:].rearrange("p (m t) -> p m t", t=PACK)
-        )
-
         z_words = sb("z_words", [S], U32)
         z_scales = sb("z_scales", [S], U8)
-        st = {}
-        for c, (a, b) in enumerate(Z_CHUNKS):
-            for nm in ("pa", "s2", "p2", "den", "num", "root", "inv"):
-                st[nm, c] = sb("%s%d" % (nm, c), [PACK, b - a], F32)
-            st["z", c] = sb("z%d" % c, [(b - a) * PACK], BF16)
+        HALF = S // 2
+        early = sb("early", [2, PACK, HALF], F32)
+        late = sb("late", [4, PACK, HALF], F32, tag="late_slot")
+        pa = [early[:, 0], late[:, 0]]
+        s_sq = [early[:, 1], late[:, 1]]
+        num = [late[:, 2], late[:, 3]]
+        pa_sq = {}
+        root = [sb("root%d" % c, [PACK * P], F32) for c in range(BLOCKS)]
+        inv = [sb("inv%d" % c, [PACK * P], F32) for c in range(BLOCKS)]
+        z = [sb("z%d" % c, [PACK * P], BF16) for c in range(BLOCKS)]
 
-        def flat(tile):
-            return tile[:].rearrange("p t c -> p (t c)")
-
-        def fetch(c):
-            a, b = Z_CHUNKS[c]
+        def fetch(h):
             for t in range(PACK):
-                nc.vector.tensor_copy(st["pa", c][:, t, :], s_win[t][:].indirect(entries(n1_sb, a, b)))
+                nc.vector.tensor_copy(pa[h][:, t, :], s_win[t][:].indirect(entries(n1_sb, halves[h][0], halves[h][1])))
 
-        def squares(c):
-            a, b = Z_CHUNKS[c]
+        def own_squares(h):
+            a, b = halves[h]
             for t in range(PACK):
-                nc.scalar.activation(st["s2", c][:, t, :], s_ps[t][:, a:b], ACT.Square, scale=SCORE_SCALE)
-            nc.scalar.activation(flat(st["p2", c]), flat(st["pa", c]), ACT.Square)
+                nc.gpsimd.tensor_tensor(s_sq[h][:, t, :], s_win[t][:, a:b], s_win[t][:, a:b], MULT)
 
-        def denominator(c):
-            nc.vector.tensor_tensor(flat(st["den", c]), flat(st["s2", c]), flat(st["p2", c]), ADD)
+        def fetched_squares(h):
+            pa_sq[h] = sb("pa_sq%d" % h, [PACK, HALF], F32)
+            for t in range(0, PACK, 2):
+                nc.scalar.activation(pa_sq[h][:, t : t + 2, :], pa[h][:, t : t + 2, :], ACT.Square)
 
-        def numerator(c):
-            a, b = Z_CHUNKS[c]
+        def add_turned(out, first, second):
+            nc.tensor.matmul(out, first, ident[:], start=True, stop=False, is_transpose=True)
+            nc.tensor.matmul(out, second, ident[:], start=False, stop=True, is_transpose=True)
+
+        def inverse_root(c):
             for t in range(PACK):
-                nc.vector.scalar_tensor_tensor(
-                    st["num", c][:, t, :], st["pa", c][:, t, :], gain[:, t : t + 1], s_ps[t][:, a:b], MULT, MULT
-                )
+                add_turned(turned_ps[c % 2][:, t, :], s_sq[c // 2][:, t, block(c % 2)], pa_sq[c // 2][:, t, block(c % 2)])
+            nc.scalar.activation(
+                root[c][:], turned_ps[c % 2][:].rearrange("p t k -> p (t k)"), ACT.Abs_reciprocal_sqrt, bias=bias_half[:]
+            )
 
         def inverse(c):
-            nc.scalar.activation(flat(st["root", c]), flat(st["den", c]), ACT.Abs_reciprocal_sqrt, bias=0.5)
-            nc.scalar.activation(flat(st["inv", c]), flat(st["root", c]), ACT.Square)
-
-        def quotient(c):
-            nc.vector.tensor_tensor(walk_out(st["z", c][:]), walk_in(st["num", c][:]), walk_in(st["inv", c][:]), MULT)
-
-        def quantise_z(c):
-            a, b = Z_CHUNKS[c]
-            nc.vector.quantize_mx(out=z_words[:, a:b].bitcast(FP8X4), scales=z_scales[:, a:b], in_=st["z", c][:])
+            nc.scalar.activation(inv[c][:], root[c][:], ACT.Square)
             for t in range(PACK):
-                cols = slice(t * P, (t + 1) * P)
-                nc.tensor.matmul_mx(
-                    out=h_ps[t][:, a:b], lhsT=value_words[:, cols].bitcast(FP8X4), lhsT_scale=value_scales[:, cols],
-                    rhs=z_words[:, a:b].bitcast(FP8X4), rhs_scale=z_scales[:, a:b], start=True, stop=True,
+                nc.tensor.transpose(back_ps[c % 2][:, t, :], inv[c][:, block(t)], ident[:])
+
+        def numerator(h):
+            a, b = halves[h]
+            for t in range(PACK):
+                nc.vector.scalar_tensor_tensor(
+                    num[h][:, t, :], pa[h][:, t, :], gain[:, t : t + 1], product_ps[t][:, a:b], MULT, MULT
                 )
 
+        def quotient(c):
+            nc.vector.tensor_tensor(walk_out(z[c][:]), walk_in(num[c // 2][:, :, block(c % 2)]), walk_in(back_ps[c % 2][:]), MULT)
+
+        def quantise_z(c):
+            nc.vector.quantize_mx(out=z_words[:, block(c)].bitcast(FP8X4), scales=z_scales[:, block(c)], in_=z[c][:])
+
+        def values(a, b):
+            for t in range(PACK):
+                nc.tensor.matmul_mx(
+                    out=product_ps[t][:, a:b], lhsT=value_words[:, block(t)].bitcast(FP8X4),
+                    lhsT_scale=value_scales[:, block(t)], rhs=z_words[:, a:b].bitcast(FP8X4), rhs_scale=z_scales[:, a:b],
+                    start=True, stop=True,
+                )
+
+        own_squares(0)
         fetch(0)
-        squares(0)
+        fetched_squares(0)
+        own_squares(1)
         fetch(1)
-        denominator(0)
-        squares(1)
-        fetch(2)
-        inverse(0)
-        denominator(1)
-        squares(2)
+        inverse_root(0)
+        inverse_root(1)
+        fetched_squares(1)
         numerator(0)
+        inverse(0)
+        inverse_root(2)
         inverse(1)
-        denominator(2)
-        quotient(0)
         numerator(1)
+        value_scales = sb("value_scales", [N], U8, tag="s_win3")
+        nc.gpsimd.tensor_copy(
+            value_scales[:].rearrange("p (t m) -> p m t", t=PACK), w_bytes_raw[:].rearrange("p (m t) -> p m t", t=PACK)
+        )
+        inverse_root(3)
+        quotient(0)
         inverse(2)
-        quantise_z(0)
-        numerator(2)
         quotient(1)
+        quantise_z(0)
+        inverse(3)
         quantise_z(1)
+        values(0, 256)
         quotient(2)
         quantise_z(2)
+        values(256, 384)
+        quotient(3)
+        quantise_z(3)
 
         h_plain = [sb("h_plain%d" % t, [S], F32) for t in range(PACK)]
 
         def h_out(t, a, b):
-            nc.scalar.activation(h_win[t][:, a:b], h_ps[t][:, a:b], ACT.Copy, scale=ROOT_OUT_SCALE)
-            nc.scalar.activation(h_plain[t][:, a:b], h_ps[t][:, a:b], ACT.Copy, scale=ROOT_OUT_SCALE)
+            nc.scalar.activation(h_win[t][:, a:b], product_ps[t][:, a:b], ACT.Copy, scale=ROOT_OUT_SCALE)
+            nc.scalar.activation(h_plain[t][:, a:b], product_ps[t][:, a:b], ACT.Copy, scale=ROOT_OUT_SCALE)
 
-        split = Z_CHUNKS[-1][0]
-        h_out(0, 0, split)
-        h_out(0, split, S)
+        h_out(0, 0, 384)
+        values(384, 512)
+        h_out(0, 384, S)
         for t in range(1, PACK):
             h_out(t, 0, S)
 
         result = sb("result", [PACK, S], F32)
+        rounded = sb("rounded", [S * PACK], BF16)
         y_words = sb("y_words", [S], U32)
         y_scales = sb("y_scales", [S], U8)
         out_rows = out_0.rearrange("(p t) j -> p t j", t=PACK)
-        pieces = [(t, 0, S) for t in range(PACK - 1)] + [(PACK - 1, a, b) for a, b in OUT_CHUNKS]
-        prod = {}
 
-        def products(i):
-            t, a, b = pieces[i]
-            third = sb("third%d" % i, [b - a], F32)
-            first = sb("first%d" % i, [b - a], F32)
-            second = sb("second%d" % i, [b - a], F32)
-            prod[i] = (first, second)
+        def products(t, a, b):
+            third = sb("third%d_%d" % (t, a), [b - a], F32)
+            first = sb("first%d_%d" % (t, a), [b - a], F32)
+            second = sb("second%d_%d" % (t, a), [b - a], F32)
             nc.vector.tensor_copy(third[:], h_win[t][:].indirect(entries(n3_sb, a, b)))
             nc.vector.tensor_tensor(first[:], h_win[t][:].indirect(entries(n2_sb, a, b)), h_plain[t][:, a:b], MULT)
-            if i > 0:
-                finish(i - 1)
             nc.vector.tensor_tensor(second[:], h_win[t][:].indirect(entries(n4_sb, a, b)), third[:], MULT)
-            if i > 0:
-                planes(i - 1)
+            return first, second
 
-        def finish(i):
-            t, a, b = pieces[i]
-            nc.vector.tensor_tensor(result[:, t, a:b], prod[i][0][:], prod[i][1][:], ADD)
-            nc.sync.dma_start(out_rows[:, t, a:b], result[:, t, a:b])
-            if t == PACK - 1:
-                prod[i, "y"] = sb("y%d" % i, [(b - a) * PACK], BF16)
-                nc.scalar.copy(walk_out(prod[i, "y"][:]), walk_in(result[:, :, a:b]))
+        for t in range(PACK - 1):
+            first, second = products(t, 0, S)
+            turned = sb("turned%d" % t, [S], F32)
+            for h, (a, b) in enumerate(halves):
+                for c in range(2):
+                    add_turned(turned_ps[h][:, c, :], first[:, block(2 * h + c)], second[:, block(2 * h + c)])
+                nc.scalar.copy(turned[:, a:b], turned_ps[h][:, 0:2, :].rearrange("p c k -> p (c k)"))
+            for h, (a, b) in enumerate(halves):
+                for c in range(2):
+                    nc.tensor.transpose(back_ps[h][:, c, :], turned[:, block(2 * h + c)], ident[:])
+                nc.scalar.copy(result[:, t, a:b], back_ps[h][:, 0:2, :].rearrange("p c k -> p (c k)"))
+            nc.scalar.dma_start(out_rows[:, t, :], result[:, t, :])
 
-        def planes(i):
-            t, a, b = pieces[i]
-            if t == PACK - 1:
-                nc.vector.quantize_mx(out=y_words[:, a:b].bitcast(FP8X4), scales=y_scales[:, a:b], in_=prod[i, "y"][:])
-                nc.sync.dma_start(words_of(out_1)[:, a:b], y_words[:, a:b].bitcast(I32))
-
-        for i in range(len(pieces)):
-            products(i)
-        finish(len(pieces) - 1)
-        planes(len(pieces) - 1)
+        last = PACK - 1
+        for a, b in OUT_CHUNKS:
+            first, second = products(last, a, b)
+            nc.vector.tensor_tensor(result[:, last, a:b], first[:], second[:], ADD)
+            nc.sync.dma_start(out_rows[:, last, a:b], result[:, last, a:b])
+            nc.scalar.copy(walk_out(rounded[:, a * PACK : b * PACK]), walk_in(result[:, :, a:b]))
+        for a, b in OUT_CHUNKS:
+            nc.vector.quantize_mx(
+                out=y_words[:, a:b].bitcast(FP8X4), scales=y_scales[:, a:b], in_=rounded[:, a * PACK : b * PACK]
+            )
+            nc.sync.dma_start(words_of(out_1)[:, a:b], y_words[:, a:b].bitcast(I32))
         for q in range(4):
             queue = nc.sync if q % 2 else nc.scalar
             queue.dma_start(out_2[0, 4 * q : 4 * q + 4, :].bitcast(I32), y_scales[32 * q : 32 * q + 4, :].bitcast(I32))

@@ -141,8 +141,9 @@ def tile_picked_keyharmdot_none_po_kernel(
             nc.vector.tensor_copy(query_words[:, a:b], x_word_table[:].bitcast(U32).indirect(entries(offs_sb, a, b)))
 
         product_ps = [psum.tile([P, S], F32, name="product_ps%d" % t) for t in range(PACK)]
-        turned_ps = [psum.tile([P, PACK, P], F32, name="turned_ps%d" % i) for i in range(2)]
-        back_ps = [psum.tile([P, PACK, P], F32, name="back_ps%d" % i) for i in range(2)]
+        turn_ps = [psum.tile([P, PACK, P], F32, name="turn_ps%d" % c) for c in range(BLOCKS)]
+        turned_ps = turn_ps[0:2]
+        back_ps = turn_ps[2:4]
         s_win = [sb("s_win%d" % t, [S], F32) for t in range(PACK)]
 
         def score(t, a, b):
@@ -171,37 +172,38 @@ def tile_picked_keyharmdot_none_po_kernel(
         pa_sq = {}
         root = [sb("root%d" % c, [PACK * P], F32) for c in range(BLOCKS)]
         inv = [sb("inv%d" % c, [PACK * P], F32) for c in range(BLOCKS)]
-        z = [sb("z%d" % c, [PACK * P], BF16) for c in range(BLOCKS)]
+        z = sb("z", [PACK * S], BF16)
 
         def fetch(h):
             for t in range(PACK):
                 nc.vector.tensor_copy(pa[h][:, t, :], s_win[t][:].indirect(entries(n1_sb, halves[h][0], halves[h][1])))
 
-        def own_squares(h):
+        def own_squares(h, tiles):
             a, b = halves[h]
-            for t in range(PACK):
+            for t in tiles:
                 nc.gpsimd.tensor_tensor(s_sq[h][:, t, :], s_win[t][:, a:b], s_win[t][:, a:b], MULT)
 
-        def fetched_squares(h):
-            pa_sq[h] = sb("pa_sq%d" % h, [PACK, HALF], F32)
-            for t in range(0, PACK, 2):
-                nc.scalar.activation(pa_sq[h][:, t : t + 2, :], pa[h][:, t : t + 2, :], ACT.Square)
+        def fetched_squares(h, pair):
+            pa_sq[h, pair] = sb("pa_sq%d%d" % (h, pair), [2, HALF], F32, tag="pa_sq_late" if pair else None)
+            nc.scalar.activation(pa_sq[h, pair][:], pa[h][:, 2 * pair : 2 * pair + 2, :], ACT.Square)
 
         def add_turned(out, first, second):
             nc.tensor.matmul(out, first, ident[:], start=True, stop=False, is_transpose=True)
             nc.tensor.matmul(out, second, ident[:], start=False, stop=True, is_transpose=True)
 
+        def denominator(c, pair):
+            for t in range(2 * pair, 2 * pair + 2):
+                add_turned(turn_ps[c][:, t, :], s_sq[c // 2][:, t, block(c % 2)], pa_sq[c // 2, pair][:, t % 2, block(c % 2)])
+
         def inverse_root(c):
-            for t in range(PACK):
-                add_turned(turned_ps[c % 2][:, t, :], s_sq[c // 2][:, t, block(c % 2)], pa_sq[c // 2][:, t, block(c % 2)])
             nc.scalar.activation(
-                root[c][:], turned_ps[c % 2][:].rearrange("p t k -> p (t k)"), ACT.Abs_reciprocal_sqrt, bias=bias_half[:]
+                root[c][:], turn_ps[c][:].rearrange("p t k -> p (t k)"), ACT.Abs_reciprocal_sqrt, bias=bias_half[:]
             )
 
         def inverse(c):
             nc.scalar.activation(inv[c][:], root[c][:], ACT.Square)
             for t in range(PACK):
-                nc.tensor.transpose(back_ps[c % 2][:, t, :], inv[c][:, block(t)], ident[:])
+                nc.tensor.transpose(turn_ps[c][:, t, :], inv[c][:, block(t)], ident[:])
 
         def numerator(h):
             a, b = halves[h]
@@ -211,61 +213,69 @@ def tile_picked_keyharmdot_none_po_kernel(
                 )
 
         def quotient(c):
-            nc.vector.tensor_tensor(walk_out(z[c][:]), walk_in(num[c // 2][:, :, block(c % 2)]), walk_in(back_ps[c % 2][:]), MULT)
+            nc.vector.tensor_tensor(walk_out(z[:, c * PACK * P : (c + 1) * PACK * P]), walk_in(num[c // 2][:, :, block(c % 2)]), walk_in(turn_ps[c][:]), MULT)
 
-        def quantise_z(c):
-            nc.vector.quantize_mx(out=z_words[:, block(c)].bitcast(FP8X4), scales=z_scales[:, block(c)], in_=z[c][:])
+        def quantise_z(a, b):
+            nc.vector.quantize_mx(out=z_words[:, a:b].bitcast(FP8X4), scales=z_scales[:, a:b], in_=z[:, a * PACK : b * PACK])
 
-        def values(a, b):
-            for t in range(PACK):
-                nc.tensor.matmul_mx(
-                    out=product_ps[t][:, a:b], lhsT=value_words[:, block(t)].bitcast(FP8X4),
-                    lhsT_scale=value_scales[:, block(t)], rhs=z_words[:, a:b].bitcast(FP8X4), rhs_scale=z_scales[:, a:b],
-                    start=True, stop=True,
-                )
+        def values(t, a, b):
+            nc.tensor.matmul_mx(
+                out=product_ps[t][:, a:b], lhsT=value_words[:, block(t)].bitcast(FP8X4),
+                lhsT_scale=value_scales[:, block(t)], rhs=z_words[:, a:b].bitcast(FP8X4), rhs_scale=z_scales[:, a:b],
+                start=True, stop=True,
+            )
 
-        own_squares(0)
+        own_squares(0, range(PACK))
         fetch(0)
-        fetched_squares(0)
-        own_squares(1)
+        for pair in range(2):
+            fetched_squares(0, pair)
+            denominator(0, pair)
+            denominator(1, pair)
+        own_squares(1, range(2))
+        for t in range(2, PACK):
+            nc.scalar.activation(s_sq[1][:, t, :], product_ps[t][:, HALF:S], ACT.Square, scale=SCORE_SCALE)
         fetch(1)
         inverse_root(0)
-        inverse_root(1)
-        fetched_squares(1)
+        for pair in range(2):
+            fetched_squares(1, pair)
+            denominator(2, pair)
+            denominator(3, pair)
         numerator(0)
-        inverse(0)
-        inverse_root(2)
-        inverse(1)
         numerator(1)
         value_scales = sb("value_scales", [N], U8, tag="s_win3")
         nc.gpsimd.tensor_copy(
             value_scales[:].rearrange("p (t m) -> p m t", t=PACK), w_bytes_raw[:].rearrange("p (m t) -> p m t", t=PACK)
         )
+        inverse_root(1)
+        inverse(0)
+        inverse_root(2)
+        inverse(1)
         inverse_root(3)
-        quotient(0)
         inverse(2)
-        quotient(1)
-        quantise_z(0)
         inverse(3)
-        quantise_z(1)
-        values(0, 256)
+        quotient(0)
+        quotient(1)
+        quantise_z(0, 256)
         quotient(2)
-        quantise_z(2)
-        values(256, 384)
+        values(0, 0, 256)
+        quantise_z(256, 384)
+        values(0, 256, 384)
         quotient(3)
-        quantise_z(3)
+        quantise_z(384, 512)
 
         h_plain = [sb("h_plain%d" % t, [S], F32) for t in range(PACK)]
 
-        def h_out(t, a, b):
-            nc.scalar.activation(h_win[t][:, a:b], product_ps[t][:, a:b], ACT.Copy, scale=ROOT_OUT_SCALE)
-            nc.scalar.activation(h_plain[t][:, a:b], product_ps[t][:, a:b], ACT.Copy, scale=ROOT_OUT_SCALE)
+        def h_copy(tile, t, a, b):
+            nc.scalar.activation(tile[:, a:b], product_ps[t][:, a:b], ACT.Copy, scale=ROOT_OUT_SCALE)
 
-        h_out(0, 0, 384)
-        values(384, 512)
-        h_out(0, 384, S)
+        h_copy(h_win[0], 0, 0, 384)
+        values(0, 384, S)
+        h_copy(h_win[0], 0, 384, S)
+        h_copy(h_plain[0], 0, 0, S)
         for t in range(1, PACK):
-            h_out(t, 0, S)
+            values(t, 0, S)
+            h_copy(h_win[t], t, 0, S)
+            h_copy(h_plain[t], t, 0, S)
 
         result = sb("result", [PACK, S], F32)
         rounded = sb("rounded", [S * PACK], BF16)
@@ -282,30 +292,55 @@ def tile_picked_keyharmdot_none_po_kernel(
             nc.vector.tensor_tensor(second[:], h_win[t][:].indirect(entries(n4_sb, a, b)), third[:], MULT)
             return first, second
 
-        for t in range(PACK - 1):
+        turned = [sb("turned%d" % t, [S], F32) for t in range(PACK - 1)]
+
+        def turn_sum(t):
             first, second = products(t, 0, S)
-            turned = sb("turned%d" % t, [S], F32)
             for h, (a, b) in enumerate(halves):
                 for c in range(2):
                     add_turned(turned_ps[h][:, c, :], first[:, block(2 * h + c)], second[:, block(2 * h + c)])
-                nc.scalar.copy(turned[:, a:b], turned_ps[h][:, 0:2, :].rearrange("p c k -> p (c k)"))
-            for h, (a, b) in enumerate(halves):
-                for c in range(2):
-                    nc.tensor.transpose(back_ps[h][:, c, :], turned[:, block(2 * h + c)], ident[:])
-                nc.scalar.copy(result[:, t, a:b], back_ps[h][:, 0:2, :].rearrange("p c k -> p (c k)"))
-            nc.scalar.dma_start(out_rows[:, t, :], result[:, t, :])
+                nc.scalar.copy(turned[t][:, a:b], turned_ps[h][:, 0:2, :].rearrange("p c k -> p (c k)"))
+
+        def turn_back(t, h):
+            a, b = halves[h]
+            for c in range(2):
+                nc.tensor.transpose(back_ps[h][:, c, :], turned[t][:, block(2 * h + c)], ident[:])
+            nc.scalar.copy(result[:, t, a:b], back_ps[h][:, 0:2, :].rearrange("p c k -> p (c k)"))
+            if h == 1:
+                nc.scalar.dma_start(out_rows[:, t, :], result[:, t, :])
 
         last = PACK - 1
-        for a, b in OUT_CHUNKS:
+
+        def last_rows(a, b):
             first, second = products(last, a, b)
             nc.vector.tensor_tensor(result[:, last, a:b], first[:], second[:], ADD)
             nc.sync.dma_start(out_rows[:, last, a:b], result[:, last, a:b])
+
+        def interleave(a, b):
             nc.scalar.copy(walk_out(rounded[:, a * PACK : b * PACK]), walk_in(result[:, :, a:b]))
-        for a, b in OUT_CHUNKS:
+
+        for t in range(last):
+            turn_sum(t)
+            turn_back(t, 0)
+            if t < last - 1:
+                turn_back(t, 1)
+        last_rows(0, 256)
+        interleave(0, 256)
+        turn_back(last - 1, 1)
+        last_rows(256, 384)
+        interleave(256, 384)
+        last_rows(384, S)
+
+        def planes(a, b):
             nc.vector.quantize_mx(
                 out=y_words[:, a:b].bitcast(FP8X4), scales=y_scales[:, a:b], in_=rounded[:, a * PACK : b * PACK]
             )
             nc.sync.dma_start(words_of(out_1)[:, a:b], y_words[:, a:b].bitcast(I32))
+
+        planes(0, 256)
+        nc.vector.tensor_copy(walk_out(rounded[:, 384 * PACK :]), walk_in(result[:, :, 384:S]))
+        planes(256, 384)
+        planes(384, S)
         for q in range(4):
             queue = nc.sync if q % 2 else nc.scalar
             queue.dma_start(out_2[0, 4 * q : 4 * q + 4, :].bitcast(I32), y_scales[32 * q : 32 * q + 4, :].bitcast(I32))

@@ -20,25 +20,37 @@ ACT = mybir.ActivationFunctionType
 
 P = 128
 PACK = 4
+QUADRANTS = 4
+BLOCKS = S // P
+HALF = S // 2
+HALVES = ((0, HALF), (HALF, S))
+LAST_BLOCK = S - P
 SCORE_SCALE = 0.0625
 ROOT_OUT_SCALE = math.sqrt(0.75)
-BLOCKS = S // P
-OUT_CHUNKS = ((0, 256), (256, 384), (384, 512))
+SQUARES_ON_GPSIMD = 2
 
 
 def words_of(dram):
     return dram[0].rearrange("p n t -> p (n t)").bitcast(I32)
 
 
-def entries(lst, a, b):
-    return lst[:, a // 16 : b // 16]
+def entries(offsets, a, b):
+    return offsets[:, a // 16 : b // 16]
 
 
-def walk_out(ap):
+def undealt(ap):
+    return ap.rearrange("p (m t) -> p m t", t=PACK)
+
+
+def dealt(ap):
+    return ap.rearrange("p (t m) -> p m t", t=PACK)
+
+
+def side_by_side(ap):
     return ap.rearrange("p (c i t) -> p c t i", i=4, t=PACK)
 
 
-def walk_in(ap):
+def by_tile(ap):
     return ap.rearrange("p t (c i) -> p c t i", i=4)
 
 
@@ -50,6 +62,7 @@ def tile_picked_keyharmdot_none_po_kernel(
     tc, x_words, x_scales, d_words, d_scales, gn, w1_words, w1_scales, offs, kidx, n1, n2, n3, n4, out_0, out_1, out_2
 ):
     nc = tc.nc
+    last = PACK - 1
     with ExitStack() as ctx:
         lists = ctx.enter_context(tc.tile_pool(name="lists", bufs=1))
         keep = ctx.enter_context(tc.tile_pool(name="keep", bufs=1))
@@ -71,41 +84,42 @@ def tile_picked_keyharmdot_none_po_kernel(
         key_scales = sb("key_scales", [H], U8)
         gn_sb = sb("gn_sb", [PACK], F32)
         ident = sb("ident", [P], F32)
-        h_win = [sb("h_win%d" % t, [2 * S if t < PACK - 1 else S], F32) for t in range(PACK)]
+        h_win = [sb("h_win%d" % t, [2 * S if t < last else S], F32) for t in range(PACK)]
 
-        warm_in = sb("warm_in", [1], F32, tag="x_words_slot")
-        warm_out = sb("warm_out", [1], F32)
-        half_src = sb("half_src", [1], F32, tag="d_words_slot")
+        four = sb("four", [1], F32, tag="x_words_buffer")
+        one = sb("one", [1], F32, tag="d_words_buffer")
+        score_scale = sb("score_scale", [1], F32, tag="late_buffer")
         bias_half = sb("bias_half", [1], F32)
         nc.gpsimd.memset(d_byte_table[:].bitcast(I32), 0)
-        nc.vector.memset(half_src[:], 0.5)
-        nc.vector.tensor_copy(bias_half[:], half_src[:])
+        nc.vector.memset(one[:], 1.0)
+        nc.vector.tensor_scalar(score_scale[:], one[:], SCORE_SCALE, None, MULT)
         nc.vector.memset(x_byte_table[:].bitcast(I32), 0)
-        nc.vector.memset(warm_in[:], 1.0)
-        score_scale = sb("score_scale", [1], F32, tag="late_slot")
-        nc.vector.memset(score_scale[:], SCORE_SCALE)
-        d_word_table = sb("d_word_table", [G], I32, tag="d_words_slot")
+        nc.vector.memset(four[:], 4.0)
+        d_word_table = sb("d_word_table", [G], I32, tag="d_words_buffer")
         nc.gpsimd.memset(key_scales[:].bitcast(I32), 0)
         nc.gpsimd.memset(w_bytes_raw[:].bitcast(I32), 0)
-        for t in range(PACK - 1):
+        for t in range(last):
             nc.vector.memset(h_win[t][:, S:], 0.0)
-
 
         nc.sync.dma_start(kidx_sb[:], kidx)
         nc.scalar.dma_start(d_byte_table[0:P:8, :].bitcast(I32), d_scales[0].bitcast(I32))
         nc.sync.dma_start(offs_sb[:], offs)
         nc.sync.dma_start(d_word_table[:], words_of(d_words))
-        for q in range(4):
+        for q in range(QUADRANTS):
             queue = nc.scalar if q == 0 else nc.sync
-            queue.dma_start(x_byte_table[32 * q : 32 * q + 4, :].bitcast(I32), x_scales[0, 4 * q : 4 * q + 4, :].bitcast(I32))
-        nc.scalar.activation(warm_out[:], warm_in[:], ACT.Abs_reciprocal_sqrt)
-        x_word_table = sb("x_word_table", [T], I32, tag="x_words_slot")
+            queue.dma_start(
+                x_byte_table[32 * q : 32 * q + 4, :].bitcast(I32), x_scales[0, 4 * q : 4 * q + 4, :].bitcast(I32)
+            )
+        nc.scalar.activation(bias_half[:], four[:], ACT.Abs_reciprocal_sqrt)
+        x_word_table = sb("x_word_table", [T], I32, tag="x_words_buffer")
         nc.scalar.dma_start(x_word_table[:], words_of(x_words))
         nc.gpsimd.dma_start(gn_sb[:], gn.rearrange("(p t) o -> p (t o)", t=PACK))
         gain = sb("gain", [PACK], F32)
         nc.gpsimd.tensor_scalar(gain[:], gn_sb[:], 2.0 * SCORE_SCALE, 0.0, MULT, ADD)
-        for q in range(4):
-            nc.gpsimd.dma_start(w_bytes_raw[32 * q : 32 * q + 4, :].bitcast(I32), w1_scales[0, 4 * q : 4 * q + 4, :].bitcast(I32))
+        for q in range(QUADRANTS):
+            nc.gpsimd.dma_start(
+                w_bytes_raw[32 * q : 32 * q + 4, :].bitcast(I32), w1_scales[0, 4 * q : 4 * q + 4, :].bitcast(I32)
+            )
         nc.sync.dma_start(n1_sb[:], n1)
         nc.sync.dma_start(n3_sb[:], n3)
         nc.sync.dma_start(n2_sb[:], n2)
@@ -115,10 +129,8 @@ def tile_picked_keyharmdot_none_po_kernel(
         d_bytes_picked = sb("d_bytes_picked", [H], U8)
         d_bytes_dealt = sb("d_bytes_dealt", [H], U8)
         nc.vector.tensor_copy(d_bytes_picked[:], d_byte_table[:].indirect(kidx_sb[:]))
-        nc.vector.tensor_copy(
-            d_bytes_dealt[:].rearrange("p (t m) -> p m t", t=PACK), d_bytes_picked[:].rearrange("p (m t) -> p m t", t=PACK)
-        )
-        for q in range(4):
+        nc.vector.tensor_copy(dealt(d_bytes_dealt[:]), undealt(d_bytes_picked[:]))
+        for q in range(QUADRANTS):
             nc.sync.dma_start(
                 key_scales[32 * q : 32 * q + 4, :].bitcast(I32), d_bytes_dealt[32 * q : 32 * q + 32 : 8, :].bitcast(I32)
             )
@@ -127,45 +139,28 @@ def tile_picked_keyharmdot_none_po_kernel(
         nc.sync.dma_start(w_words_raw[:], words_of(w1_words))
         d_words_picked = sb("d_words_picked", [H], U32)
         key_words = sb("key_words", [H], U32)
-        nc.vector.tensor_copy(d_words_picked[:], d_word_table[:].bitcast(U32).indirect(kidx_sb[:]))
         query_scales = sb("query_scales", [S], U8)
-        nc.vector.tensor_copy(query_scales[:], x_byte_table[:].indirect(offs_sb[:]))
-        nc.vector.tensor_copy(
-            key_words[:].bitcast(I32).rearrange("p (t m) -> p m t", t=PACK),
-            d_words_picked[:].bitcast(I32).rearrange("p (m t) -> p m t", t=PACK),
-        )
-
         query_words = sb("query_words", [S], U32)
-        halves = ((0, S // 2), (S // 2, S))
-        for a, b in halves:
-            nc.vector.tensor_copy(query_words[:, a:b], x_word_table[:].bitcast(U32).indirect(entries(offs_sb, a, b)))
+        nc.vector.tensor_copy(d_words_picked[:], d_word_table[:].bitcast(U32).indirect(kidx_sb[:]))
+        nc.vector.tensor_copy(query_scales[:], x_byte_table[:].indirect(offs_sb[:]))
+        nc.vector.tensor_copy(dealt(key_words[:].bitcast(I32)), undealt(d_words_picked[:].bitcast(I32)))
+        nc.vector.tensor_copy(query_words[:], x_word_table[:].bitcast(U32).indirect(offs_sb[:]))
 
         product_ps = [psum.tile([P, S], F32, name="product_ps%d" % t) for t in range(PACK)]
         turn_ps = [psum.tile([P, PACK, P], F32, name="turn_ps%d" % c) for c in range(BLOCKS)]
-        turned_ps = turn_ps[0:2]
-        back_ps = turn_ps[2:4]
         s_win = [sb("s_win%d" % t, [S], F32) for t in range(PACK)]
-
-        def score(t, a, b):
+        for t in range(PACK):
             nc.tensor.matmul_mx(
-                out=product_ps[t][:, a:b], lhsT=key_words[:, block(t)].bitcast(FP8X4), lhsT_scale=key_scales[:, block(t)],
-                rhs=query_words[:, a:b].bitcast(FP8X4), rhs_scale=query_scales[:, a:b], start=True, stop=True,
+                out=product_ps[t][:], lhsT=key_words[:, block(t)].bitcast(FP8X4), lhsT_scale=key_scales[:, block(t)],
+                rhs=query_words[:].bitcast(FP8X4), rhs_scale=query_scales[:], start=True, stop=True,
             )
-            nc.scalar.activation(s_win[t][:, a:b], product_ps[t][:, a:b], ACT.Copy, scale=score_scale[:])
+            nc.scalar.activation(s_win[t][:], product_ps[t][:], ACT.Copy, scale=score_scale[:])
 
-        for t, half in ((0, 0), (1, 0), (0, 1), (1, 1), (2, 0), (2, 1), (3, 0), (3, 1)):
-            score(t, halves[half][0], halves[half][1])
+        value_words = sb("value_words", [N], U32, tag="x_words_buffer")
+        nc.vector.tensor_copy(dealt(value_words[:].bitcast(I32)), undealt(w_words_raw[:]))
 
-        value_words = sb("value_words", [N], U32, tag="x_words_slot")
-        nc.vector.tensor_copy(
-            value_words[:].bitcast(I32).rearrange("p (t m) -> p m t", t=PACK),
-            w_words_raw[:].rearrange("p (m t) -> p m t", t=PACK),
-        )
-        z_words = sb("z_words", [S], U32)
-        z_scales = sb("z_scales", [S], U8)
-        HALF = S // 2
         early = sb("early", [2, PACK, HALF], F32)
-        late = sb("late", [4, PACK, HALF], F32, tag="late_slot")
+        late = sb("late", [4, PACK, HALF], F32, tag="late_buffer")
         pa = [early[:, 0], late[:, 0]]
         s_sq = [early[:, 1], late[:, 1]]
         num = [late[:, 2], late[:, 3]]
@@ -173,27 +168,32 @@ def tile_picked_keyharmdot_none_po_kernel(
         root = [sb("root%d" % c, [PACK * P], F32) for c in range(BLOCKS)]
         inv = [sb("inv%d" % c, [PACK * P], F32) for c in range(BLOCKS)]
         z = sb("z", [PACK * S], BF16)
+        z_words = sb("z_words", [S], U32)
+        z_scales = sb("z_scales", [S], U8)
 
         def fetch(h):
+            a, b = HALVES[h]
             for t in range(PACK):
-                nc.vector.tensor_copy(pa[h][:, t, :], s_win[t][:].indirect(entries(n1_sb, halves[h][0], halves[h][1])))
+                nc.vector.tensor_copy(pa[h][:, t, :], s_win[t][:].indirect(entries(n1_sb, a, b)))
 
         def own_squares(h, tiles):
-            a, b = halves[h]
+            a, b = HALVES[h]
             for t in tiles:
                 nc.gpsimd.tensor_tensor(s_sq[h][:, t, :], s_win[t][:, a:b], s_win[t][:, a:b], MULT)
-
-        def fetched_squares(h, pair):
-            pa_sq[h, pair] = sb("pa_sq%d%d" % (h, pair), [2, HALF], F32, tag="pa_sq_late" if pair else None)
-            nc.scalar.activation(pa_sq[h, pair][:], pa[h][:, 2 * pair : 2 * pair + 2, :], ACT.Square)
 
         def add_turned(out, first, second):
             nc.tensor.matmul(out, first, ident[:], start=True, stop=False, is_transpose=True)
             nc.tensor.matmul(out, second, ident[:], start=False, stop=True, is_transpose=True)
 
-        def denominator(c, pair):
-            for t in range(2 * pair, 2 * pair + 2):
-                add_turned(turn_ps[c][:, t, :], s_sq[c // 2][:, t, block(c % 2)], pa_sq[c // 2, pair][:, t % 2, block(c % 2)])
+        def denominators(h):
+            for pair in range(2):
+                pa_sq[h, pair] = sb("pa_sq%d%d" % (h, pair), [2, HALF], F32, tag="pa_sq_upper" if pair else None)
+                nc.scalar.activation(pa_sq[h, pair][:], pa[h][:, 2 * pair : 2 * pair + 2, :], ACT.Square)
+                for i in range(2):
+                    for t in range(2 * pair, 2 * pair + 2):
+                        add_turned(
+                            turn_ps[2 * h + i][:, t, :], s_sq[h][:, t, block(i)], pa_sq[h, pair][:, t % 2, block(i)]
+                        )
 
         def inverse_root(c):
             nc.scalar.activation(
@@ -206,130 +206,110 @@ def tile_picked_keyharmdot_none_po_kernel(
                 nc.tensor.transpose(turn_ps[c][:, t, :], inv[c][:, block(t)], ident[:])
 
         def numerator(h):
-            a, b = halves[h]
+            a, b = HALVES[h]
             for t in range(PACK):
                 nc.vector.scalar_tensor_tensor(
                     num[h][:, t, :], pa[h][:, t, :], gain[:, t : t + 1], product_ps[t][:, a:b], MULT, MULT
                 )
 
         def quotient(c):
-            nc.vector.tensor_tensor(walk_out(z[:, c * PACK * P : (c + 1) * PACK * P]), walk_in(num[c // 2][:, :, block(c % 2)]), walk_in(turn_ps[c][:]), MULT)
+            nc.vector.tensor_tensor(
+                side_by_side(z[:, c * PACK * P : (c + 1) * PACK * P]),
+                by_tile(num[c // 2][:, :, block(c % 2)]),
+                by_tile(turn_ps[c][:]),
+                MULT,
+            )
 
         def quantise_z(a, b):
-            nc.vector.quantize_mx(out=z_words[:, a:b].bitcast(FP8X4), scales=z_scales[:, a:b], in_=z[:, a * PACK : b * PACK])
-
-        def values(t, a, b):
-            nc.tensor.matmul_mx(
-                out=product_ps[t][:, a:b], lhsT=value_words[:, block(t)].bitcast(FP8X4),
-                lhsT_scale=value_scales[:, block(t)], rhs=z_words[:, a:b].bitcast(FP8X4), rhs_scale=z_scales[:, a:b],
-                start=True, stop=True,
+            nc.vector.quantize_mx(
+                out=z_words[:, a:b].bitcast(FP8X4), scales=z_scales[:, a:b], in_=z[:, a * PACK : b * PACK]
             )
 
         own_squares(0, range(PACK))
         fetch(0)
-        for pair in range(2):
-            fetched_squares(0, pair)
-            denominator(0, pair)
-            denominator(1, pair)
-        own_squares(1, range(2))
-        for t in range(2, PACK):
+        denominators(0)
+        own_squares(1, range(SQUARES_ON_GPSIMD))
+        for t in range(SQUARES_ON_GPSIMD, PACK):
             nc.scalar.activation(s_sq[1][:, t, :], product_ps[t][:, HALF:S], ACT.Square, scale=SCORE_SCALE)
         fetch(1)
         inverse_root(0)
-        for pair in range(2):
-            fetched_squares(1, pair)
-            denominator(2, pair)
-            denominator(3, pair)
+        denominators(1)
         numerator(0)
         numerator(1)
-        value_scales = sb("value_scales", [N], U8, tag="s_win3")
-        nc.gpsimd.tensor_copy(
-            value_scales[:].rearrange("p (t m) -> p m t", t=PACK), w_bytes_raw[:].rearrange("p (m t) -> p m t", t=PACK)
-        )
-        inverse_root(1)
-        inverse(0)
-        inverse_root(2)
-        inverse(1)
-        inverse_root(3)
-        inverse(2)
-        inverse(3)
-        quotient(0)
-        quotient(1)
-        quantise_z(0, 256)
-        quotient(2)
-        values(0, 0, 256)
-        quantise_z(256, 384)
-        values(0, 256, 384)
-        quotient(3)
-        quantise_z(384, 512)
+        value_scales = sb("value_scales", [N], U8, tag="s_win%d" % last)
+        nc.gpsimd.tensor_copy(dealt(value_scales[:]), undealt(w_bytes_raw[:]))
+        for c in range(1, BLOCKS):
+            inverse_root(c)
+            inverse(c - 1)
+        inverse(BLOCKS - 1)
+
+        def values(out, t, a, b):
+            nc.tensor.matmul_mx(
+                out=out, lhsT=value_words[:, block(t)].bitcast(FP8X4), lhsT_scale=value_scales[:, block(t)],
+                rhs=z_words[:, a:b].bitcast(FP8X4), rhs_scale=z_scales[:, a:b], start=True, stop=True,
+            )
+
+        def h_copy(out, bank):
+            nc.scalar.activation(out, bank, ACT.Copy, scale=ROOT_OUT_SCALE)
 
         h_plain = [sb("h_plain%d" % t, [S], F32) for t in range(PACK)]
-
-        def h_copy(tile, t, a, b):
-            nc.scalar.activation(tile[:, a:b], product_ps[t][:, a:b], ACT.Copy, scale=ROOT_OUT_SCALE)
-
-        h_copy(h_win[0], 0, 0, 384)
-        values(0, 384, S)
-        h_copy(h_win[0], 0, 384, S)
-        h_copy(h_plain[0], 0, 0, S)
+        quotient(0)
+        quotient(1)
+        quantise_z(0, HALF)
+        quotient(2)
+        values(product_ps[0][:, 0:HALF], 0, 0, HALF)
+        quantise_z(HALF, LAST_BLOCK)
+        values(product_ps[0][:, HALF:LAST_BLOCK], 0, HALF, LAST_BLOCK)
+        quotient(3)
+        quantise_z(LAST_BLOCK, S)
+        h_copy(h_win[0][:, 0:LAST_BLOCK], product_ps[0][:, 0:LAST_BLOCK])
+        values(turn_ps[0][:, 0, :], 0, LAST_BLOCK, S)
+        h_copy(h_win[0][:, LAST_BLOCK:S], turn_ps[0][:, 0, :])
+        h_copy(h_plain[0][:, 0:LAST_BLOCK], product_ps[0][:, 0:LAST_BLOCK])
+        h_copy(h_plain[0][:, LAST_BLOCK:S], turn_ps[0][:, 0, :])
         for t in range(1, PACK):
-            values(t, 0, S)
-            h_copy(h_win[t], t, 0, S)
-            h_copy(h_plain[t], t, 0, S)
+            values(product_ps[t][:], t, 0, S)
+            h_copy(h_win[t][:, 0:S], product_ps[t][:])
+            h_copy(h_plain[t][:], product_ps[t][:])
 
         result = sb("result", [PACK, S], F32)
         rounded = sb("rounded", [S * PACK], BF16)
         y_words = sb("y_words", [S], U32)
         y_scales = sb("y_scales", [S], U8)
+        turned = [sb("turned%d" % t, [S], F32) for t in range(last)]
         out_rows = out_0.rearrange("(p t) j -> p t j", t=PACK)
 
         def products(t, a, b):
-            third = sb("third%d_%d" % (t, a), [b - a], F32)
+            h_at_n3 = sb("h_at_n3_%d_%d" % (t, a), [b - a], F32)
             first = sb("first%d_%d" % (t, a), [b - a], F32)
             second = sb("second%d_%d" % (t, a), [b - a], F32)
-            nc.vector.tensor_copy(third[:], h_win[t][:].indirect(entries(n3_sb, a, b)))
+            nc.vector.tensor_copy(h_at_n3[:], h_win[t][:].indirect(entries(n3_sb, a, b)))
             nc.vector.tensor_tensor(first[:], h_win[t][:].indirect(entries(n2_sb, a, b)), h_plain[t][:, a:b], MULT)
-            nc.vector.tensor_tensor(second[:], h_win[t][:].indirect(entries(n4_sb, a, b)), third[:], MULT)
+            nc.vector.tensor_tensor(second[:], h_win[t][:].indirect(entries(n4_sb, a, b)), h_at_n3[:], MULT)
             return first, second
-
-        turned = [sb("turned%d" % t, [S], F32) for t in range(PACK - 1)]
 
         def turn_sum(t):
             first, second = products(t, 0, S)
-            for h, (a, b) in enumerate(halves):
-                for c in range(2):
-                    add_turned(turned_ps[h][:, c, :], first[:, block(2 * h + c)], second[:, block(2 * h + c)])
-                nc.scalar.copy(turned[t][:, a:b], turned_ps[h][:, 0:2, :].rearrange("p c k -> p (c k)"))
+            for h, (a, b) in enumerate(HALVES):
+                for i in range(2):
+                    add_turned(turn_ps[h][:, i, :], first[:, block(2 * h + i)], second[:, block(2 * h + i)])
+                nc.scalar.copy(turned[t][:, a:b], turn_ps[h][:, 0:2, :].rearrange("p c k -> p (c k)"))
 
         def turn_back(t, h):
-            a, b = halves[h]
-            for c in range(2):
-                nc.tensor.transpose(back_ps[h][:, c, :], turned[t][:, block(2 * h + c)], ident[:])
-            nc.scalar.copy(result[:, t, a:b], back_ps[h][:, 0:2, :].rearrange("p c k -> p (c k)"))
+            a, b = HALVES[h]
+            for i in range(2):
+                nc.tensor.transpose(turn_ps[2 + h][:, i, :], turned[t][:, block(2 * h + i)], ident[:])
+            nc.scalar.copy(result[:, t, a:b], turn_ps[2 + h][:, 0:2, :].rearrange("p c k -> p (c k)"))
             if h == 1:
                 nc.scalar.dma_start(out_rows[:, t, :], result[:, t, :])
-
-        last = PACK - 1
 
         def last_rows(a, b):
             first, second = products(last, a, b)
             nc.vector.tensor_tensor(result[:, last, a:b], first[:], second[:], ADD)
             nc.sync.dma_start(out_rows[:, last, a:b], result[:, last, a:b])
 
-        def interleave(a, b):
-            nc.scalar.copy(walk_out(rounded[:, a * PACK : b * PACK]), walk_in(result[:, :, a:b]))
-
-        for t in range(last):
-            turn_sum(t)
-            turn_back(t, 0)
-            if t < last - 1:
-                turn_back(t, 1)
-        last_rows(0, 256)
-        interleave(0, 256)
-        turn_back(last - 1, 1)
-        last_rows(256, 384)
-        interleave(256, 384)
-        last_rows(384, S)
+        def round_on_scalar(a, b):
+            nc.scalar.copy(side_by_side(rounded[:, a * PACK : b * PACK]), by_tile(result[:, :, a:b]))
 
         def planes(a, b):
             nc.vector.quantize_mx(
@@ -337,10 +317,22 @@ def tile_picked_keyharmdot_none_po_kernel(
             )
             nc.sync.dma_start(words_of(out_1)[:, a:b], y_words[:, a:b].bitcast(I32))
 
-        planes(0, 256)
-        nc.vector.tensor_copy(walk_out(rounded[:, 384 * PACK :]), walk_in(result[:, :, 384:S]))
-        planes(256, 384)
-        planes(384, S)
-        for q in range(4):
+        for t in range(last - 1):
+            turn_sum(t)
+            turn_back(t, 0)
+            turn_back(t, 1)
+        turn_sum(last - 1)
+        turn_back(last - 1, 0)
+        last_rows(0, HALF)
+        round_on_scalar(0, HALF)
+        turn_back(last - 1, 1)
+        last_rows(HALF, LAST_BLOCK)
+        round_on_scalar(HALF, LAST_BLOCK)
+        last_rows(LAST_BLOCK, S)
+        planes(0, HALF)
+        nc.vector.tensor_copy(side_by_side(rounded[:, LAST_BLOCK * PACK :]), by_tile(result[:, :, LAST_BLOCK:S]))
+        planes(HALF, LAST_BLOCK)
+        planes(LAST_BLOCK, S)
+        for q in range(QUADRANTS):
             queue = nc.sync if q % 2 else nc.scalar
             queue.dma_start(out_2[0, 4 * q : 4 * q + 4, :].bitcast(I32), y_scales[32 * q : 32 * q + 4, :].bitcast(I32))

import math
from contextlib import ExitStack

import concourse.mybir as mybir
from concourse.masks import make_identity

K, T, S, N, G, H = 512, 2048, 512, 512, 2048, 512
FLOPS = 2 * K * H * S + 2 * H * N * S

F32 = mybir.dt.float32
BF16 = mybir.dt.bfloat16
I32 = mybir.dt.int32
U32 = mybir.dt.uint32
U16 = mybir.dt.uint16
U8 = mybir.dt.uint8
FP8X4 = mybir.dt.float8_e4m3fn_x4
MULT = mybir.AluOpType.mult
ADD = mybir.AluOpType.add
ACT = mybir.ActivationFunctionType

P = 128
PACK = 4
QUADRANTS = 4
BLOCKS = S // P
HALF = S // 2
HALVES = ((0, HALF), (HALF, S))
LAST_BLOCK = S - P
SCORE_SCALE = 0.0625
ROOT_OUT_SCALE = math.sqrt(0.75)
SQUARES_ON_GPSIMD = 2


def words_of(dram):
    return dram[0].rearrange("p n t -> p (n t)").bitcast(I32)


def entries(offsets, a, b):
    return offsets[:, a // 16 : b // 16]


def undealt(ap):
    return ap.rearrange("p (m t) -> p m t", t=PACK)


def dealt(ap):
    return ap.rearrange("p (t m) -> p m t", t=PACK)


def side_by_side(ap):
    return ap.rearrange("p (c i t) -> p c t i", i=4, t=PACK)


def by_tile(ap):
    return ap.rearrange("p t (c i) -> p c t i", i=4)


def block(c):
    return slice(c * P, (c + 1) * P)


def tile_picked_keyharmdot_none_po_kernel(
    tc, x_words, x_scales, d_words, d_scales, gn, w1_words, w1_scales, offs, kidx, n1, n2, n3, n4, out_0, out_1, out_2
):
    nc = tc.nc
    last = PACK - 1
    with ExitStack() as ctx:
        lists = ctx.enter_context(tc.tile_pool(name="lists", bufs=1))
        keep = ctx.enter_context(tc.tile_pool(name="keep", bufs=1))
        psum = ctx.enter_context(tc.psum_pool(name="psum", bufs=1))

        def sb(name, cols, dtype, tag=None):
            return keep.tile([P] + list(cols), dtype, name=name, tag=tag or name, align_bytes=64)

        kidx_sb = lists.tile([P, H // 16], U16, name="kidx_sb")
        offs_sb = lists.tile([P, S // 16], U16, name="offs_sb")
        n1_sb = lists.tile([P, S // 16], U16, name="n1_sb")
        n2_sb = lists.tile([P, S // 16], U16, name="n2_sb")
        n3_sb = lists.tile([P, S // 16], U16, name="n3_sb")
        n4_sb = lists.tile([P, S // 16], U16, name="n4_sb")

        d_byte_table = sb("d_byte_table", [G], U8)
        x_byte_table = sb("x_byte_table", [T], U8)
        w_bytes_raw = sb("w_bytes_raw", [N], U8)
        key_scales = sb("key_scales", [H], U8)
        gn_sb = sb("gn_sb", [PACK], F32)
        ident = sb("ident", [P], F32)
        h_win = [sb("h_win%d" % t, [2 * S if t < last else S], F32) for t in range(PACK)]

        four = sb("four", [1], F32, tag="x_words_buffer")
        one = sb("one", [1], F32, tag="d_words_buffer")
        score_scale = sb("score_scale", [1], F32, tag="late_buffer")
        bias_half = sb("bias_half", [1], F32)
        nc.gpsimd.memset(d_byte_table[:].bitcast(I32), 0)
        nc.vector.memset(one[:], 1.0)
        nc.vector.tensor_scalar(score_scale[:], one[:], SCORE_SCALE, None, MULT)
        nc.vector.memset(x_byte_table[:].bitcast(I32), 0)
        nc.vector.memset(four[:], 4.0)
        d_word_table = sb("d_word_table", [G], I32, tag="d_words_buffer")
        nc.gpsimd.memset(key_scales[:].bitcast(I32), 0)
        nc.gpsimd.memset(w_bytes_raw[:].bitcast(I32), 0)
        for t in range(last):
            nc.vector.memset(h_win[t][:, S:], 0.0)

        nc.sync.dma_start(kidx_sb[:], kidx)
        nc.scalar.dma_start(d_byte_table[0:P:8, :].bitcast(I32), d_scales[0].bitcast(I32))
        nc.sync.dma_start(offs_sb[:], offs)
        nc.sync.dma_start(d_word_table[:], words_of(d_words))
        for q in range(QUADRANTS):
            queue = nc.scalar if q == 0 else nc.sync
            queue.dma_start(
                x_byte_table[32 * q : 32 * q + 4, :].bitcast(I32), x_scales[0, 4 * q : 4 * q + 4, :].bitcast(I32)
            )
        nc.scalar.activation(bias_half[:], four[:], ACT.Abs_reciprocal_sqrt)
        x_word_table = sb("x_word_table", [T], I32, tag="x_words_buffer")
        nc.scalar.dma_start(x_word_table[:], words_of(x_words))
        nc.gpsimd.dma_start(gn_sb[:], gn.rearrange("(p t) o -> p (t o)", t=PACK))
        gain = sb("gain", [PACK], F32)
        nc.gpsimd.tensor_scalar(gain[:], gn_sb[:], 2.0 * SCORE_SCALE, 0.0, MULT, ADD)
        for q in range(QUADRANTS):
            nc.gpsimd.dma_start(
                w_bytes_raw[32 * q : 32 * q + 4, :].bitcast(I32), w1_scales[0, 4 * q : 4 * q + 4, :].bitcast(I32)
            )
        nc.sync.dma_start(n1_sb[:], n1)
        nc.sync.dma_start(n3_sb[:], n3)
        nc.sync.dma_start(n2_sb[:], n2)
        nc.sync.dma_start(n4_sb[:], n4)
        make_identity(nc, ident[:])

        d_bytes_picked = sb("d_bytes_picked", [H], U8)
        d_bytes_dealt = sb("d_bytes_dealt", [H], U8)
        nc.vector.tensor_copy(d_bytes_picked[:], d_byte_table[:].indirect(kidx_sb[:]))
        nc.vector.tensor_copy(dealt(d_bytes_dealt[:]), undealt(d_bytes_picked[:]))
        for q in range(QUADRANTS):
            nc.sync.dma_start(
                key_scales[32 * q : 32 * q + 4, :].bitcast(I32), d_bytes_dealt[32 * q : 32 * q + 32 : 8, :].bitcast(I32)
            )

        w_words_raw = sb("w_words_raw", [N], I32, tag="d_bytes_picked")
        nc.sync.dma_start(w_words_raw[:], words_of(w1_words))
        d_words_picked = sb("d_words_picked", [H], U32)
        key_words = sb("key_words", [H], U32)
        query_scales = sb("query_scales", [S], U8)
        query_words = sb("query_words", [S], U32)
        nc.vector.tensor_copy(d_words_picked[:], d_word_table[:].bitcast(U32).indirect(kidx_sb[:]))
        nc.vector.tensor_copy(query_scales[:], x_byte_table[:].indirect(offs_sb[:]))
        nc.vector.tensor_copy(dealt(key_words[:].bitcast(I32)), undealt(d_words_picked[:].bitcast(I32)))
        nc.vector.tensor_copy(query_words[:], x_word_table[:].bitcast(U32).indirect(offs_sb[:]))

        product_ps = [psum.tile([P, S], F32, name="product_ps%d" % t) for t in range(PACK)]
        turn_ps = [psum.tile([P, PACK, P], F32, name="turn_ps%d" % c) for c in range(BLOCKS)]
        s_win = [sb("s_win%d" % t, [S], F32) for t in range(PACK)]
        for t in range(PACK):
            nc.tensor.matmul_mx(
                out=product_ps[t][:], lhsT=key_words[:, block(t)].bitcast(FP8X4), lhsT_scale=key_scales[:, block(t)],
                rhs=query_words[:].bitcast(FP8X4), rhs_scale=query_scales[:], start=True, stop=True,
            )
            nc.scalar.activation(s_win[t][:], product_ps[t][:], ACT.Copy, scale=score_scale[:])

        value_words = sb("value_words", [N], U32, tag="x_words_buffer")
        nc.vector.tensor_copy(dealt(value_words[:].bitcast(I32)), undealt(w_words_raw[:]))

        early = sb("early", [2, PACK, HALF], F32)
        late = sb("late", [4, PACK, HALF], F32, tag="late_buffer")
        pa = [early[:, 0], late[:, 0]]
        s_sq = [early[:, 1], late[:, 1]]
        num = [late[:, 2], late[:, 3]]
        pa_sq = {}
        root = [sb("root%d" % c, [PACK * P], F32) for c in range(BLOCKS)]
        inv = [sb("inv%d" % c, [PACK * P], F32) for c in range(BLOCKS)]
        z = sb("z", [PACK * S], BF16)
        z_words = sb("z_words", [S], U32)
        z_scales = sb("z_scales", [S], U8)

        def fetch(h):
            a, b = HALVES[h]
            for t in range(PACK):
                nc.vector.tensor_copy(pa[h][:, t, :], s_win[t][:].indirect(entries(n1_sb, a, b)))

        def own_squares(h, tiles):
            a, b = HALVES[h]
            for t in tiles:
                nc.gpsimd.tensor_tensor(s_sq[h][:, t, :], s_win[t][:, a:b], s_win[t][:, a:b], MULT)

        def add_turned(out, first, second):
            nc.tensor.matmul(out, first, ident[:], start=True, stop=False, is_transpose=True)
            nc.tensor.matmul(out, second, ident[:], start=False, stop=True, is_transpose=True)

        def denominators(h):
            for pair in range(2):
                pa_sq[h, pair] = sb("pa_sq%d%d" % (h, pair), [2, HALF], F32, tag="pa_sq_upper" if pair else None)
                nc.scalar.activation(pa_sq[h, pair][:], pa[h][:, 2 * pair : 2 * pair + 2, :], ACT.Square)
                for i in range(2):
                    for t in range(2 * pair, 2 * pair + 2):
                        add_turned(
                            turn_ps[2 * h + i][:, t, :], s_sq[h][:, t, block(i)], pa_sq[h, pair][:, t % 2, block(i)]
                        )

        def inverse_root(c):
            nc.scalar.activation(
                root[c][:], turn_ps[c][:].rearrange("p t k -> p (t k)"), ACT.Abs_reciprocal_sqrt, bias=bias_half[:]
            )

        def inverse(c):
            nc.scalar.activation(inv[c][:], root[c][:], ACT.Square)
            for t in range(PACK):
                nc.tensor.transpose(turn_ps[c][:, t, :], inv[c][:, block(t)], ident[:])

        def numerator(h):
            a, b = HALVES[h]
            for t in range(PACK):
                nc.vector.scalar_tensor_tensor(
                    num[h][:, t, :], pa[h][:, t, :], gain[:, t : t + 1], product_ps[t][:, a:b], MULT, MULT
                )

        def quotient(c):
            nc.vector.tensor_tensor(
                side_by_side(z[:, c * PACK * P : (c + 1) * PACK * P]),
                by_tile(num[c // 2][:, :, block(c % 2)]),
                by_tile(turn_ps[c][:]),
                MULT,
            )

        def quantise_z(a, b):
            nc.vector.quantize_mx(
                out=z_words[:, a:b].bitcast(FP8X4), scales=z_scales[:, a:b], in_=z[:, a * PACK : b * PACK]
            )

        own_squares(0, range(PACK))
        fetch(0)
        denominators(0)
        own_squares(1, range(SQUARES_ON_GPSIMD))
        for t in range(SQUARES_ON_GPSIMD, PACK):
            nc.scalar.activation(s_sq[1][:, t, :], product_ps[t][:, HALF:S], ACT.Square, scale=SCORE_SCALE)
        fetch(1)
        inverse_root(0)
        denominators(1)
        numerator(0)
        numerator(1)
        value_scales = sb("value_scales", [N], U8, tag="s_win%d" % last)
        nc.gpsimd.tensor_copy(dealt(value_scales[:]), undealt(w_bytes_raw[:]))
        for c in range(1, BLOCKS):
            inverse_root(c)
            inverse(c - 1)
        inverse(BLOCKS - 1)

        def values(out, t, a, b):
            nc.tensor.matmul_mx(
                out=out, lhsT=value_words[:, block(t)].bitcast(FP8X4), lhsT_scale=value_scales[:, block(t)],
                rhs=z_words[:, a:b].bitcast(FP8X4), rhs_scale=z_scales[:, a:b], start=True, stop=True,
            )

        def h_copy(out, bank):
            nc.scalar.activation(out, bank, ACT.Copy, scale=ROOT_OUT_SCALE)

        h_plain = [sb("h_plain%d" % t, [S], F32) for t in range(PACK)]
        quotient(0)
        quotient(1)
        quantise_z(0, HALF)
        quotient(2)
        values(product_ps[0][:, 0:HALF], 0, 0, HALF)
        quantise_z(HALF, LAST_BLOCK)
        values(product_ps[0][:, HALF:LAST_BLOCK], 0, HALF, LAST_BLOCK)
        quotient(3)
        quantise_z(LAST_BLOCK, S)
        h_copy(h_win[0][:, 0:LAST_BLOCK], product_ps[0][:, 0:LAST_BLOCK])
        values(turn_ps[0][:, 0, :], 0, LAST_BLOCK, S)
        h_copy(h_win[0][:, LAST_BLOCK:S], turn_ps[0][:, 0, :])
        h_copy(h_plain[0][:, 0:LAST_BLOCK], product_ps[0][:, 0:LAST_BLOCK])
        h_copy(h_plain[0][:, LAST_BLOCK:S], turn_ps[0][:, 0, :])
        for t in range(1, PACK):
            values(product_ps[t][:], t, 0, S)
            h_copy(h_win[t][:, 0:S], product_ps[t][:])
            h_copy(h_plain[t][:], product_ps[t][:])

        result = sb("result", [PACK, S], F32)
        rounded = sb("rounded", [S * PACK], BF16)
        y_words = sb("y_words", [S], U32)
        y_scales = sb("y_scales", [S], U8)
        turned = [sb("turned%d" % t, [S], F32) for t in range(last)]
        out_rows = out_0.rearrange("(p t) j -> p t j", t=PACK)

        def products(t, a, b):
            h_at_n3 = sb("h_at_n3_%d_%d" % (t, a), [b - a], F32)
            first = sb("first%d_%d" % (t, a), [b - a], F32)
            second = sb("second%d_%d" % (t, a), [b - a], F32)
            nc.vector.tensor_copy(h_at_n3[:], h_win[t][:].indirect(entries(n3_sb, a, b)))
            nc.vector.tensor_tensor(first[:], h_win[t][:].indirect(entries(n2_sb, a, b)), h_plain[t][:, a:b], MULT)
            nc.vector.tensor_tensor(second[:], h_win[t][:].indirect(entries(n4_sb, a, b)), h_at_n3[:], MULT)
            return first, second

        def turn_sum(t):
            first, second = products(t, 0, S)
            for h, (a, b) in enumerate(HALVES):
                for i in range(2):
                    add_turned(turn_ps[h][:, i, :], first[:, block(2 * h + i)], second[:, block(2 * h + i)])
                nc.scalar.copy(turned[t][:, a:b], turn_ps[h][:, 0:2, :].rearrange("p c k -> p (c k)"))

        def turn_back(t, h):
            a, b = HALVES[h]
            for i in range(2):
                nc.tensor.transpose(turn_ps[2 + h][:, i, :], turned[t][:, block(2 * h + i)], ident[:])
            nc.scalar.copy(result[:, t, a:b], turn_ps[2 + h][:, 0:2, :].rearrange("p c k -> p (c k)"))
            if h == 1:
                nc.scalar.dma_start(out_rows[:, t, :], result[:, t, :])

        def last_rows(a, b):
            first, second = products(last, a, b)
            nc.vector.tensor_tensor(result[:, last, a:b], first[:], second[:], ADD)
            nc.sync.dma_start(out_rows[:, last, a:b], result[:, last, a:b])

        def round_on_scalar(a, b):
            nc.scalar.copy(side_by_side(rounded[:, a * PACK : b * PACK]), by_tile(result[:, :, a:b]))

        def planes(a, b):
            nc.vector.quantize_mx(
                out=y_words[:, a:b].bitcast(FP8X4), scales=y_scales[:, a:b], in_=rounded[:, a * PACK : b * PACK]
            )
            nc.sync.dma_start(words_of(out_1)[:, a:b], y_words[:, a:b].bitcast(I32))

        for t in range(last - 1):
            turn_sum(t)
            turn_back(t, 0)
            turn_back(t, 1)
        turn_sum(last - 1)
        turn_back(last - 1, 0)
        last_rows(0, HALF)
        round_on_scalar(0, HALF)
        turn_back(last - 1, 1)
        last_rows(HALF, LAST_BLOCK)
        round_on_scalar(HALF, LAST_BLOCK)
        last_rows(LAST_BLOCK, S)
        planes(0, HALF)
        nc.vector.tensor_copy(side_by_side(rounded[:, LAST_BLOCK * PACK :]), by_tile(result[:, :, LAST_BLOCK:S]))
        planes(HALF, LAST_BLOCK)
        planes(LAST_BLOCK, S)
        for q in range(QUADRANTS):
            queue = nc.sync if q % 2 else nc.scalar
            queue.dma_start(out_2[0, 4 * q : 4 * q + 4, :].bitcast(I32), y_scales[32 * q : 32 * q + 4, :].bitcast(I32))
